import numpy as np
import ml_dtypes


def mxq(x, axis, fmt="e4m3"):
    dtype, down = {"e4m3": (ml_dtypes.float8_e4m3fn, 7), "e5m2": (ml_dtypes.float8_e5m2, 14)}[fmt]
    v = np.moveaxis(np.asarray(x, np.float32).astype(ml_dtypes.bfloat16).astype(np.float64), axis, -1)
    blocks = v.reshape(v.shape[:-1] + (-1, 32))
    amax = np.abs(blocks).max(-1, keepdims=True)
    byte = np.maximum(np.where(amax > 0, np.frexp(amax)[1] - 1 + 127, 0) - down, 1)
    scale = np.exp2(byte - 127.0)
    codes = (blocks / scale).astype(np.float32).astype(dtype).astype(np.float64)
    return np.moveaxis((codes * scale).reshape(v.shape), -1, axis)


WIDE = False


def mx_kscale(k):
    if not WIDE:
        return np.ones(k)
    levels = np.array([10, -10, 5, -5, 0])
    if k % 512:
        return np.exp2(np.random.permutation(np.resize(levels, k // 32))).repeat(32)
    a = np.empty((k // 512, 16))
    for p in range(k // 512):
        a[p, :8] = np.random.permutation(np.resize(levels, 8))
        for g in range(8):
            far = levels[np.abs(levels - a[p, g]) >= 10]
            a[p, g + 8] = far[np.random.randint(len(far))]
    return np.exp2(a.ravel()).repeat(32)


def f64(x):
    return np.asarray(x).astype(np.float64)


def striped8(idx):
    return np.asarray(idx).reshape(8, -1, 16).transpose(0, 2, 1).reshape(128, -1).astype(np.uint16)


def unstriped8(offs):
    return offs.reshape(8, 16, -1).transpose(0, 2, 1).reshape(8, -1).astype(np.int64)


def pick8(x, idx, run):
    r = np.arange(len(x))
    return x[r[:, None], idx[r % (8 * run) // run]]


E2M1 = np.array([0.0, 0.5, 1.0, 1.5, 2.0, 3.0, 4.0, 6.0, -0.0, -0.5, -1.0, -1.5, -2.0, -3.0, -4.0, -6.0])


def pack_weight(w, fmt):
    k, n = w.shape
    w = f64(np.asarray(w, np.float32).astype(ml_dtypes.bfloat16)).reshape(k // 32, 32, n)
    amax = np.abs(w).max(1)
    if fmt == "e4m3":
        byte = np.frexp(amax)[1] - 1 + 127 - 7
    else:
        mant, ex = np.frexp(amax / 6.0)
        byte = np.where(mant > 0.5, ex, ex - 1) + 127
    byte = np.clip(np.where(amax > 0, byte, 1), 1, 254)
    scaled = (w * np.exp2(127.0 - byte)[:, None, :]).reshape(k, n).astype(np.float32)
    by_word = np.ascontiguousarray(scaled.reshape(k // 512, 128, 4, n).transpose(0, 1, 3, 2))
    if fmt == "e4m3":
        words = by_word.astype(ml_dtypes.float8_e4m3fn).view(np.uint8)
    else:
        c = by_word.astype(ml_dtypes.float4_e2m1fn).view(np.uint8) & 0xF
        words = (c[..., 0::2] | (c[..., 1::2] << 4)).reshape(k // 512, 128, 2 * n)
    return np.ascontiguousarray(words), np.ascontiguousarray(byte.astype(np.uint8).reshape(k // 512, 16, n))


def unpack_weight(words, scales, fmt):
    g, _, n = scales.shape
    words = np.ascontiguousarray(words).reshape(g, 128, n, -1)
    if fmt == "e4m3":
        vals = words.view(ml_dtypes.float8_e4m3fn).astype(np.float64)
    else:
        nib = np.empty((g, 128, n, 4), np.uint8)
        nib[..., 0::2] = words & 0xF
        nib[..., 1::2] = words >> 4
        vals = E2M1[nib]
    vals = vals * np.repeat(np.exp2(scales.astype(np.float64) - 127.0), 8, axis=1)[..., None]
    return vals.transpose(0, 1, 3, 2).reshape(g * 512, n)


def sigmoid(v):
    return 1.0 / (1.0 + np.exp(-v))


K, T, J, N = 512, 512, 512, 512


def setup_inputs():
    n = np.random.standard_normal
    idx = np.stack([np.random.randint(0, T, J) for _ in range(8)])
    idx2 = np.stack([np.random.randint(0, T, J) for _ in range(8)])
    fk = mx_kscale(K)
    xtp = pack_weight(n((K, T)) / fk[:, None], "e4m3")
    wvp = pack_weight(n((K, N)) * 1 / np.sqrt(K) * fk[:, None], "e2m1")
    return {
        "xt_words": xtp[0],
        "xt_scales": xtp[1],
        "wv_words": wvp[0],
        "wv_scales": wvp[1],
        "wg": (n((K, N)) * 1 / np.sqrt(K) * fk[:, None]).astype(np.float32),
        "offs": striped8(idx),
        "offs2": striped8(idx2),
    }


def reference(xt_words, xt_scales, wv_words, wv_scales, wg, offs, offs2):
    idx = unstriped8(offs)
    idx2 = unstriped8(offs2)
    xtu = unpack_weight(xt_words, xt_scales, "e4m3")
    wvu = unpack_weight(wv_words, wv_scales, "e2m1")
    v = wvu.T @ xtu
    wgq = mxq(f64(wg), 0, "e4m3")
    g = wgq.T @ xtu
    y = pick8(v, idx, 64) * sigmoid(pick8(g, idx2, 64))
    return y

@@ -1,0 +1,155 @@
+from contextlib import ExitStack
+
+import concourse.mybir as mybir
+
+K, T, J, N = 512, 512, 512, 512
+FLOPS = 2 * 2 * K * N * T
+
+F32 = mybir.dt.float32
+BF16 = mybir.dt.bfloat16
+I32 = mybir.dt.int32
+U32 = mybir.dt.uint32
+U16 = mybir.dt.uint16
+U8 = mybir.dt.uint8
+FP8X4 = mybir.dt.float8_e4m3fn_x4
+FP4X4 = mybir.dt.float4_e2m1fn_x4
+SIGMOID = mybir.ActivationFunctionType.Sigmoid
+MULT = mybir.AluOpType.mult
+
+P = 128
+PACK = 4
+TILES = N // P
+RUN = 4
+WG_PIECES = (256, 128, 128)
+WINDOW = 2 * T
+
+
+def tile_list_head_gate_from_other_token_kernel(tc, xt_words, xt_scales, wv_words, wv_scales, wg, offs, offs2, out):
+    nc = tc.nc
+    with ExitStack() as ctx:
+        keep = ctx.enter_context(tc.tile_pool(name="keep", bufs=1))
+        psum = ctx.enter_context(tc.psum_pool(name="psum", bufs=1))
+
+        warm_in = keep.tile([P, 1], F32)
+        warm_out = keep.tile([P, 1], F32)
+        ws_raw = keep.tile([P, N], U8, align_bytes=64)
+        xs = keep.tile([P, T], U8, align_bytes=64)
+        nc.vector.memset(ws_raw[:].bitcast(I32), 0)
+        nc.vector.memset(xs[:].bitcast(I32), 0)
+        nc.gpsimd.memset(warm_in[:], 0.0)
+        nc.scalar.activation(warm_out[:], warm_in[:], SIGMOID)
+
+        wv_raw = keep.tile([P, 2 * N], U8, align_bytes=64)
+        nc.sync.dma_start(wv_raw[:].bitcast(I32), wv_words[0].bitcast(I32))
+        for q in range(4):
+            nc.sync.dma_start(ws_raw[32 * q : 32 * q + 4, :].bitcast(I32), wv_scales[0, 4 * q : 4 * q + 4, :].bitcast(I32))
+        xt = keep.tile([P, T], U32, align_bytes=64)
+        nc.sync.dma_start(xt[:].bitcast(I32), xt_words[0].rearrange("p t r -> p (t r)").bitcast(I32))
+        wg_rows = wg.rearrange("(p j) n -> p j n", j=PACK)
+        wg_raw = []
+        n0 = 0
+        for i, width in enumerate(WG_PIECES):
+            piece = keep.tile([P, PACK, width], F32, name=f"wg_raw{i}")
+            nc.sync.dma_start(piece[:], wg_rows[:, :, n0 : n0 + width])
+            wg_raw.append((piece, n0, width))
+            n0 = n0 + width
+            if i == 1:
+                for q in range(4):
+                    nc.scalar.dma_start(xs[32 * q : 32 * q + 4, :].bitcast(I32), xt_scales[0, 4 * q : 4 * q + 4, :].bitcast(I32))
+        gate_list = keep.tile([P, J // 16], U16)
+        nc.sync.dma_start(gate_list[:], offs2)
+        value_list = keep.tile([P, J // 16], U16)
+        nc.sync.dma_start(value_list[:], offs)
+
+        wv = keep.tile([P, 2 * N], U8, align_bytes=64)
+        ws = keep.tile([P, N], U8, align_bytes=64)
+        nc.vector.tensor_copy(
+            wv[:].bitcast(I32).rearrange("p (b a w) -> p b a w", b=TILES, w=2),
+            wv_raw[:].bitcast(I32).rearrange("p (a b w) -> p b a w", b=TILES, w=2),
+        )
+        nc.vector.tensor_copy(
+            ws[:].bitcast(I32).rearrange("p (b a) -> p b a", b=TILES),
+            ws_raw[:].bitcast(I32).rearrange("p (a b) -> p b a", b=TILES),
+        )
+
+        v_tiles = []
+        for b in range(TILES):
+            acc = psum.tile([P, T], F32, name=f"v_acc{b}")
+            nc.tensor.matmul_mx(
+                out=acc[:],
+                lhsT=wv[:, 2 * P * b : 2 * P * (b + 1)].bitcast(FP4X4),
+                lhsT_scale=ws[:, P * b : P * (b + 1)],
+                rhs=xt[:].bitcast(FP8X4),
+                rhs_scale=xs[:],
+                start=True,
+                stop=True,
+            )
+            v = keep.tile([P, WINDOW], F32, name=f"v{b}")
+            nc.scalar.copy(v[:, 0:T], acc[:])
+            v_tiles.append(v)
+
+        grouped = keep.tile([P, TILES, P, PACK], BF16, align_bytes=64)
+        for piece, n0, width in wg_raw:
+            m0 = n0 // TILES
+            nc.vector.tensor_copy(
+                grouped[:, :, m0 : m0 + width // TILES, :].rearrange("p b (a c) j -> p b a j c", c=RUN),
+                piece[:].rearrange("p j (a b c) -> p b a j c", b=TILES, c=RUN),
+            )
+
+        wg_mx = []
+        for b in range(TILES):
+            codes = keep.tile([P, P], U32, name=f"wg_codes{b}", align_bytes=64)
+            scales = keep.tile([P, P], U8, name=f"wg_scales{b}", align_bytes=64)
+            nc.vector.quantize_mx(
+                out=codes[:].bitcast(FP8X4),
+                scales=scales[:],
+                in_=grouped[:, b, :, :].rearrange("p m j -> p (m j)"),
+            )
+            wg_mx.append((codes, scales))
+
+        def gate_product(acc, b, cols):
+            codes, scales = wg_mx[b]
+            nc.tensor.matmul_mx(
+                out=acc,
+                lhsT=codes[:].bitcast(FP8X4),
+                lhsT_scale=scales[:],
+                rhs=xt[:, cols].bitcast(FP8X4),
+                rhs_scale=xs[:, cols],
+                start=True,
+                stop=True,
+            )
+
+        half = T // 2
+        g0_low = psum.tile([P, T], F32, name="g0_low", tag="v_acc0")
+        g0_high = psum.tile([P, T], F32, name="g0_high")
+        gate_product(g0_low[:, 0:half], 0, slice(0, half))
+        gate_product(g0_high[:, 0:half], 0, slice(half, T))
+        g_accs = [None]
+        for b in range(1, TILES):
+            acc = psum.tile([P, T], F32, name=f"g_acc{b}")
+            gate_product(acc[:], b, slice(0, T))
+            g_accs.append(acc)
+
+        out_rows = out.rearrange("(a b c) j -> b a c j", b=TILES, c=RUN)
+        gates = []
+        for b in range(TILES):
+            g = keep.tile([P, WINDOW], F32, name=f"g{b}", tag=f"g{min(b, 2)}")
+            if b == 0:
+                nc.vector.tensor_copy(g[:, 0:half], g0_low[:, 0:half])
+                nc.scalar.copy(g[:, half:T], g0_high[:, 0:half])
+            elif b < TILES - 1:
+                nc.vector.tensor_copy(g[:, 0:T], g_accs[b][:])
+            else:
+                nc.scalar.copy(g[:, 0:T], g_accs[b][:])
+            pieces = 2 if b == TILES - 1 else 1
+            width = J // pieces
+            for i in range(pieces):
+                gate = keep.tile([P, width], F32, name=f"gate{b}_{i}")
+                entries = slice(i * width // 16, (i + 1) * width // 16)
+                nc.scalar.activation(gate[:], g[:].indirect(gate_list[:, entries]), SIGMOID)
+                gates.append((b, gate, i * width, width))
+        for b, gate, j0, width in gates:
+            y = keep.tile([P, width], F32, name=f"y{b}_{j0}")
+            entries = slice(j0 // 16, (j0 + width) // 16)
+            nc.vector.tensor_tensor(y[:], v_tiles[b][:].indirect(value_list[:, entries]), gate[:], MULT)
+            nc.sync.dma_start(out_rows[b, :, :, j0 : j0 + width], y[:])

@@ -20,7 +20,8 @@ P = 128
 PACK = 4
 TILES = N // P
 RUN = 4
-WG_PIECES = (256, 128, 128)
+HALF = N // 2
+QUARTER = N // 4
 WINDOW = 2 * T
 
 
@@ -32,124 +33,140 @@ def tile_list_head_gate_from_other_token_kernel(tc, xt_words, xt_scales, wv_word
 
         warm_in = keep.tile([P, 1], F32)
         warm_out = keep.tile([P, 1], F32)
+        wv_raw = keep.tile([P, 2 * N], U8, align_bytes=64)
         ws_raw = keep.tile([P, N], U8, align_bytes=64)
+        wv_words_raw = wv_raw[:].bitcast(I32)
+        wv_scales_raw = ws_raw[:].bitcast(I32)
         xs = keep.tile([P, T], U8, align_bytes=64)
-        nc.vector.memset(ws_raw[:].bitcast(I32), 0)
-        nc.vector.memset(xs[:].bitcast(I32), 0)
+        nc.vector.memset(wv_scales_raw, 0)
         nc.gpsimd.memset(warm_in[:], 0.0)
         nc.scalar.activation(warm_out[:], warm_in[:], SIGMOID)
 
-        wv_raw = keep.tile([P, 2 * N], U8, align_bytes=64)
-        nc.sync.dma_start(wv_raw[:].bitcast(I32), wv_words[0].bitcast(I32))
+        wg_rows = wg.rearrange("(p j) n -> p j n", j=PACK)
+        wg_first = keep.tile([P, PACK, QUARTER], F32)
+        nc.sync.dma_start(wg_first[:], wg_rows[:, :, 0:QUARTER])
         for q in range(4):
-            nc.sync.dma_start(ws_raw[32 * q : 32 * q + 4, :].bitcast(I32), wv_scales[0, 4 * q : 4 * q + 4, :].bitcast(I32))
+            nc.sync.dma_start(xs[32 * q : 32 * q + 4, :].bitcast(I32), xt_scales[0, 4 * q : 4 * q + 4, :].bitcast(I32))
+        wg_second = keep.tile([P, PACK, QUARTER], F32)
+        nc.sync.dma_start(wg_second[:], wg_rows[:, :, QUARTER:HALF])
+        wg_high = keep.tile([P, PACK, HALF], F32)
+        nc.sync.dma_start(wg_high[:], wg_rows[:, :, HALF:N])
         xt = keep.tile([P, T], U32, align_bytes=64)
         nc.sync.dma_start(xt[:].bitcast(I32), xt_words[0].rearrange("p t r -> p (t r)").bitcast(I32))
-        wg_rows = wg.rearrange("(p j) n -> p j n", j=PACK)
-        wg_raw = []
-        n0 = 0
-        for i, width in enumerate(WG_PIECES):
-            piece = keep.tile([P, PACK, width], F32, name=f"wg_raw{i}")
-            nc.sync.dma_start(piece[:], wg_rows[:, :, n0 : n0 + width])
-            wg_raw.append((piece, n0, width))
-            n0 = n0 + width
-            if i == 1:
-                for q in range(4):
-                    nc.scalar.dma_start(xs[32 * q : 32 * q + 4, :].bitcast(I32), xt_scales[0, 4 * q : 4 * q + 4, :].bitcast(I32))
+        for q in range(4):
+            nc.sync.dma_start(wv_scales_raw[32 * q : 32 * q + 4, :], wv_scales[0, 4 * q : 4 * q + 4, :].bitcast(I32))
+        nc.sync.dma_start(wv_words_raw, wv_words[0].bitcast(I32))
         gate_list = keep.tile([P, J // 16], U16)
         nc.sync.dma_start(gate_list[:], offs2)
         value_list = keep.tile([P, J // 16], U16)
         nc.sync.dma_start(value_list[:], offs)
 
+        wg_codes = [keep.tile([P, P], U32, name=f"wg_codes{b}", align_bytes=64) for b in range(TILES)]
+        wg_scales = [keep.tile([P, P], U8, name=f"wg_scales{b}", align_bytes=64) for b in range(TILES)]
+
+        def interleave(copy, pieces, b0, b1, name):
+            grouped = keep.tile([P, b1 - b0, P // 2, PACK], BF16, name=name, align_bytes=64)
+            width = P // 2 // len(pieces)
+            for i, raw in enumerate(pieces):
+                copy(
+                    grouped[:, :, i * width : (i + 1) * width, :].rearrange("p b (a c) j -> p b a j c", c=RUN),
+                    raw[:].rearrange("p j (a b c) -> p b a j c", b=TILES, c=RUN)[:, b0:b1],
+                )
+            return [grouped[:, b, :, :].rearrange("p m j -> p (m j)") for b in range(b1 - b0)]
+
+        def quantize(grouped, m0):
+            cols = slice(m0, m0 + P // 2)
+            for b in range(TILES):
+                nc.vector.quantize_mx(out=wg_codes[b][:, cols].bitcast(FP8X4), scales=wg_scales[b][:, cols], in_=grouped[b])
+
+        quantize(interleave(nc.vector.tensor_copy, [wg_first, wg_second], 0, TILES, "grouped_low"), 0)
+        quantize(
+            interleave(nc.vector.tensor_copy, [wg_high], 0, 1, "grouped_high0")
+            + interleave(nc.vector.tensor_copy, [wg_high], 1, 2, "grouped_high1")
+            + interleave(nc.scalar.copy, [wg_high], 2, TILES, "grouped_high23"),
+            P // 2,
+        )
+
         wv = keep.tile([P, 2 * N], U8, align_bytes=64)
         ws = keep.tile([P, N], U8, align_bytes=64)
-        nc.vector.tensor_copy(
-            wv[:].bitcast(I32).rearrange("p (b a w) -> p b a w", b=TILES, w=2),
-            wv_raw[:].bitcast(I32).rearrange("p (a b w) -> p b a w", b=TILES, w=2),
-        )
-        nc.vector.tensor_copy(
+        nc.gpsimd.tensor_copy(
             ws[:].bitcast(I32).rearrange("p (b a) -> p b a", b=TILES),
-            ws_raw[:].bitcast(I32).rearrange("p (a b) -> p b a", b=TILES),
+            wv_scales_raw.rearrange("p (a b) -> p b a", b=TILES),
+        )
+        nc.gpsimd.tensor_copy(
+            wv[:].bitcast(I32).rearrange("p (b a w) -> p b a w", b=TILES, w=2),
+            wv_words_raw.rearrange("p (a b w) -> p b a w", b=TILES, w=2),
         )
 
-        v_tiles = []
-        for b in range(TILES):
-            acc = psum.tile([P, T], F32, name=f"v_acc{b}")
-            nc.tensor.matmul_mx(
-                out=acc[:],
-                lhsT=wv[:, 2 * P * b : 2 * P * (b + 1)].bitcast(FP4X4),
-                lhsT_scale=ws[:, P * b : P * (b + 1)],
-                rhs=xt[:].bitcast(FP8X4),
-                rhs_scale=xs[:],
-                start=True,
-                stop=True,
-            )
-            v = keep.tile([P, WINDOW], F32, name=f"v{b}")
-            nc.scalar.copy(v[:, 0:T], acc[:])
-            v_tiles.append(v)
-
-        grouped = keep.tile([P, TILES, P, PACK], BF16, align_bytes=64)
-        for piece, n0, width in wg_raw:
-            m0 = n0 // TILES
-            nc.vector.tensor_copy(
-                grouped[:, :, m0 : m0 + width // TILES, :].rearrange("p b (a c) j -> p b a j c", c=RUN),
-                piece[:].rearrange("p j (a b c) -> p b a j c", b=TILES, c=RUN),
-            )
-
-        wg_mx = []
-        for b in range(TILES):
-            codes = keep.tile([P, P], U32, name=f"wg_codes{b}", align_bytes=64)
-            scales = keep.tile([P, P], U8, name=f"wg_scales{b}", align_bytes=64)
-            nc.vector.quantize_mx(
-                out=codes[:].bitcast(FP8X4),
-                scales=scales[:],
-                in_=grouped[:, b, :, :].rearrange("p m j -> p (m j)"),
-            )
-            wg_mx.append((codes, scales))
-
-        def gate_product(acc, b, cols):
-            codes, scales = wg_mx[b]
+        def product(acc, lhsT, lhsT_scale, cols):
             nc.tensor.matmul_mx(
                 out=acc,
-                lhsT=codes[:].bitcast(FP8X4),
-                lhsT_scale=scales[:],
+                lhsT=lhsT,
+                lhsT_scale=lhsT_scale,
                 rhs=xt[:, cols].bitcast(FP8X4),
                 rhs_scale=xs[:, cols],
                 start=True,
                 stop=True,
             )
 
+        def gate_product(acc, b, cols):
+            product(acc, wg_codes[b][:].bitcast(FP8X4), wg_scales[b][:], cols)
+
+        def value_product(acc, b, cols):
+            product(acc, wv[:, 2 * P * b : 2 * P * (b + 1)].bitcast(FP4X4), ws[:, P * b : P * (b + 1)], cols)
+
         half = T // 2
-        g0_low = psum.tile([P, T], F32, name="g0_low", tag="v_acc0")
+        g0_low = psum.tile([P, T], F32, name="g0_low", tag="shared_bank")
         g0_high = psum.tile([P, T], F32, name="g0_high")
         gate_product(g0_low[:, 0:half], 0, slice(0, half))
         gate_product(g0_high[:, 0:half], 0, slice(half, T))
-        g_accs = [None]
-        for b in range(1, TILES):
-            acc = psum.tile([P, T], F32, name=f"g_acc{b}")
+        g0 = keep.tile([P, WINDOW], F32, name="g0", tag="g_even", align_bytes=64)
+        nc.scalar.copy(g0[:, 0:half], g0_low[:, 0:half])
+        nc.vector.tensor_copy(g0[:, half:T], g0_high[:, 0:half])
+
+        def gate_bank(b, tag):
+            acc = psum.tile([P, T], F32, name=f"g_acc{b}", tag=tag)
             gate_product(acc[:], b, slice(0, T))
-            g_accs.append(acc)
+            return acc
+
+        def value_bank(b, tag):
+            acc = psum.tile([P, T], F32, name=f"v_acc{b}", tag=tag)
+            value_product(acc[:], b, slice(0, T))
+            return acc
+
+        def window(copy, acc, name, tag):
+            tile = keep.tile([P, WINDOW], F32, name=name, tag=tag, align_bytes=64)
+            copy(tile[:, 0:T], acc[:])
+            return tile
 
         out_rows = out.rearrange("(a b c) j -> b a c j", b=TILES, c=RUN)
-        gates = []
-        for b in range(TILES):
-            g = keep.tile([P, WINDOW], F32, name=f"g{b}", tag=f"g{min(b, 2)}")
-            if b == 0:
-                nc.vector.tensor_copy(g[:, 0:half], g0_low[:, 0:half])
-                nc.scalar.copy(g[:, half:T], g0_high[:, 0:half])
-            elif b < TILES - 1:
-                nc.vector.tensor_copy(g[:, 0:T], g_accs[b][:])
-            else:
-                nc.scalar.copy(g[:, 0:T], g_accs[b][:])
-            pieces = 2 if b == TILES - 1 else 1
-            width = J // pieces
-            for i in range(pieces):
-                gate = keep.tile([P, width], F32, name=f"gate{b}_{i}")
-                entries = slice(i * width // 16, (i + 1) * width // 16)
-                nc.scalar.activation(gate[:], g[:].indirect(gate_list[:, entries]), SIGMOID)
-                gates.append((b, gate, i * width, width))
-        for b, gate, j0, width in gates:
+
+        def gather_gate(g, b, j0, width):
+            gate = keep.tile([P, width], F32, name=f"gate{b}_{j0}")
+            nc.scalar.activation(gate[:], g[:].indirect(gate_list[:, j0 // 16 : (j0 + width) // 16]), SIGMOID)
+            return gate
+
+        def gather_value(v, gate, b, j0, width):
             y = keep.tile([P, width], F32, name=f"y{b}_{j0}")
-            entries = slice(j0 // 16, (j0 + width) // 16)
-            nc.vector.tensor_tensor(y[:], v_tiles[b][:].indirect(value_list[:, entries]), gate[:], MULT)
+            nc.vector.tensor_tensor(y[:], v[:].indirect(value_list[:, j0 // 16 : (j0 + width) // 16]), gate[:], MULT)
             nc.sync.dma_start(out_rows[b, :, :, j0 : j0 + width], y[:])
+
+        g1 = window(nc.vector.tensor_copy, gate_bank(1, "g_acc1"), "g1", "g_odd")
+        v = [window(nc.vector.tensor_copy, value_bank(b, f"v_acc{b}"), f"v{b}", f"v{b}") for b in range(3)]
+        gate0 = gather_gate(g0, 0, 0, J)
+        gate1 = gather_gate(g1, 1, 0, J)
+        gather_value(v[0], gate0, 0, 0, J)
+        g2 = window(nc.scalar.copy, gate_bank(2, "v_acc0"), "g2", "g_even")
+        g3 = window(nc.scalar.copy, gate_bank(3, "v_acc1"), "g3", "g_odd")
+        gather_value(v[1], gate1, 1, 0, J)
+        gate2 = gather_gate(g2, 2, 0, J)
+        v3_low = psum.tile([P, T], F32, name="v3_low", tag="v_acc2")
+        v3_high = psum.tile([P, T], F32, name="v3_high", tag="v_acc0")
+        value_product(v3_low[:, 0:half], 3, slice(0, half))
+        value_product(v3_high[:, 0:half], 3, slice(half, T))
+        v3 = keep.tile([P, WINDOW], F32, name="v3", tag="v0", align_bytes=64)
+        nc.scalar.copy(v3[:, 0:half], v3_low[:, 0:half])
+        nc.vector.tensor_copy(v3[:, half:T], v3_high[:, 0:half])
+        gather_value(v[2], gate2, 2, 0, J)
+        for j0 in (0, half):
+            gather_value(v3, gather_gate(g3, 3, j0, half), 3, j0, half)

@@ -33,10 +33,9 @@ def tile_list_head_gate_from_other_token_kernel(tc, xt_words, xt_scales, wv_word
 
         warm_in = keep.tile([P, 1], F32)
         warm_out = keep.tile([P, 1], F32)
-        wv_raw = keep.tile([P, 2 * N], U8, align_bytes=64)
-        ws_raw = keep.tile([P, N], U8, align_bytes=64)
-        wv_words_raw = wv_raw[:].bitcast(I32)
-        wv_scales_raw = ws_raw[:].bitcast(I32)
+        wv_raw = keep.tile([P, 3 * N], U8, align_bytes=64, tag="g_odd")
+        wv_words_raw = wv_raw[:, 0 : 2 * N].bitcast(I32)
+        wv_scales_raw = wv_raw[:, 2 * N : 3 * N].bitcast(I32)
         xs = keep.tile([P, T], U8, align_bytes=64)
         nc.vector.memset(wv_scales_raw, 0)
         nc.gpsimd.memset(warm_in[:], 0.0)
@@ -89,13 +88,13 @@ def tile_list_head_gate_from_other_token_kernel(tc, xt_words, xt_scales, wv_word
 
         wv = keep.tile([P, 2 * N], U8, align_bytes=64)
         ws = keep.tile([P, N], U8, align_bytes=64)
-        nc.gpsimd.tensor_copy(
-            ws[:].bitcast(I32).rearrange("p (b a) -> p b a", b=TILES),
-            wv_scales_raw.rearrange("p (a b) -> p b a", b=TILES),
-        )
-        nc.gpsimd.tensor_copy(
+        nc.vector.tensor_copy(
             wv[:].bitcast(I32).rearrange("p (b a w) -> p b a w", b=TILES, w=2),
             wv_words_raw.rearrange("p (a b w) -> p b a w", b=TILES, w=2),
+        )
+        nc.vector.tensor_copy(
+            ws[:].bitcast(I32).rearrange("p (b a) -> p b a", b=TILES),
+            wv_scales_raw.rearrange("p (a b) -> p b a", b=TILES),
         )
 
         def product(acc, lhsT, lhsT_scale, cols):
@@ -122,7 +121,7 @@ def tile_list_head_gate_from_other_token_kernel(tc, xt_words, xt_scales, wv_word
         gate_product(g0_high[:, 0:half], 0, slice(half, T))
         g0 = keep.tile([P, WINDOW], F32, name="g0", tag="g_even", align_bytes=64)
         nc.scalar.copy(g0[:, 0:half], g0_low[:, 0:half])
-        nc.vector.tensor_copy(g0[:, half:T], g0_high[:, 0:half])
+        nc.scalar.copy(g0[:, half:T], g0_high[:, 0:half])
 
         def gate_bank(b, tag):
             acc = psum.tile([P, T], F32, name=f"g_acc{b}", tag=tag)
@@ -160,13 +159,7 @@ def tile_list_head_gate_from_other_token_kernel(tc, xt_words, xt_scales, wv_word
         g3 = window(nc.scalar.copy, gate_bank(3, "v_acc1"), "g3", "g_odd")
         gather_value(v[1], gate1, 1, 0, J)
         gate2 = gather_gate(g2, 2, 0, J)
-        v3_low = psum.tile([P, T], F32, name="v3_low", tag="v_acc2")
-        v3_high = psum.tile([P, T], F32, name="v3_high", tag="v_acc0")
-        value_product(v3_low[:, 0:half], 3, slice(0, half))
-        value_product(v3_high[:, 0:half], 3, slice(half, T))
-        v3 = keep.tile([P, WINDOW], F32, name="v3", tag="v0", align_bytes=64)
-        nc.scalar.copy(v3[:, 0:half], v3_low[:, 0:half])
-        nc.vector.tensor_copy(v3[:, half:T], v3_high[:, 0:half])
+        v3 = window(nc.scalar.copy, value_bank(3, "v_acc2"), "v3", "v0")
         gather_value(v[2], gate2, 2, 0, J)
         for j0 in (0, half):
             gather_value(v3, gather_gate(g3, 3, j0, half), 3, j0, half)

from contextlib import ExitStack

import concourse.mybir as mybir

K, T, J, N = 512, 512, 512, 512
FLOPS = 2 * 2 * K * N * T

F32 = mybir.dt.float32
BF16 = mybir.dt.bfloat16
I32 = mybir.dt.int32
U32 = mybir.dt.uint32
U16 = mybir.dt.uint16
U8 = mybir.dt.uint8
FP8X4 = mybir.dt.float8_e4m3fn_x4
FP4X4 = mybir.dt.float4_e2m1fn_x4
SIGMOID = mybir.ActivationFunctionType.Sigmoid
MULT = mybir.AluOpType.mult

P = 128
PACK = 4
TILES = N // P
RUN = 4
HALF = N // 2
QUARTER = N // 4
WINDOW = 2 * T


def tile_list_head_gate_from_other_token_kernel(tc, xt_words, xt_scales, wv_words, wv_scales, wg, offs, offs2, out):
    nc = tc.nc
    with ExitStack() as ctx:
        keep = ctx.enter_context(tc.tile_pool(name="keep", bufs=1))
        psum = ctx.enter_context(tc.psum_pool(name="psum", bufs=1))

        warm_in = keep.tile([P, 1], F32)
        warm_out = keep.tile([P, 1], F32)
        wv_raw = keep.tile([P, 3 * N], U8, align_bytes=64, tag="g_odd")
        wv_words_raw = wv_raw[:, 0 : 2 * N].bitcast(I32)
        wv_scales_raw = wv_raw[:, 2 * N : 3 * N].bitcast(I32)
        xs = keep.tile([P, T], U8, align_bytes=64)
        nc.vector.memset(wv_scales_raw, 0)
        nc.gpsimd.memset(warm_in[:], 0.0)
        nc.scalar.activation(warm_out[:], warm_in[:], SIGMOID)

        wg_rows = wg.rearrange("(p j) n -> p j n", j=PACK)
        wg_first = keep.tile([P, PACK, QUARTER], F32)
        nc.sync.dma_start(wg_first[:], wg_rows[:, :, 0:QUARTER])
        for q in range(4):
            nc.sync.dma_start(xs[32 * q : 32 * q + 4, :].bitcast(I32), xt_scales[0, 4 * q : 4 * q + 4, :].bitcast(I32))
        wg_second = keep.tile([P, PACK, QUARTER], F32)
        nc.sync.dma_start(wg_second[:], wg_rows[:, :, QUARTER:HALF])
        wg_high = keep.tile([P, PACK, HALF], F32)
        nc.sync.dma_start(wg_high[:], wg_rows[:, :, HALF:N])
        xt = keep.tile([P, T], U32, align_bytes=64)
        nc.sync.dma_start(xt[:].bitcast(I32), xt_words[0].rearrange("p t r -> p (t r)").bitcast(I32))
        for q in range(4):
            nc.sync.dma_start(wv_scales_raw[32 * q : 32 * q + 4, :], wv_scales[0, 4 * q : 4 * q + 4, :].bitcast(I32))
        nc.sync.dma_start(wv_words_raw, wv_words[0].bitcast(I32))
        gate_list = keep.tile([P, J // 16], U16)
        nc.sync.dma_start(gate_list[:], offs2)
        value_list = keep.tile([P, J // 16], U16)
        nc.sync.dma_start(value_list[:], offs)

        wg_codes = [keep.tile([P, P], U32, name=f"wg_codes{b}", align_bytes=64) for b in range(TILES)]
        wg_scales = [keep.tile([P, P], U8, name=f"wg_scales{b}", align_bytes=64) for b in range(TILES)]

        def interleave(copy, pieces, b0, b1, name):
            grouped = keep.tile([P, b1 - b0, P // 2, PACK], BF16, name=name, align_bytes=64)
            width = P // 2 // len(pieces)
            for i, raw in enumerate(pieces):
                copy(
                    grouped[:, :, i * width : (i + 1) * width, :].rearrange("p b (a c) j -> p b a j c", c=RUN),
                    raw[:].rearrange("p j (a b c) -> p b a j c", b=TILES, c=RUN)[:, b0:b1],
                )
            return [grouped[:, b, :, :].rearrange("p m j -> p (m j)") for b in range(b1 - b0)]

        def quantize(grouped, m0):
            cols = slice(m0, m0 + P // 2)
            for b in range(TILES):
                nc.vector.quantize_mx(out=wg_codes[b][:, cols].bitcast(FP8X4), scales=wg_scales[b][:, cols], in_=grouped[b])

        quantize(interleave(nc.vector.tensor_copy, [wg_first, wg_second], 0, TILES, "grouped_low"), 0)
        quantize(
            interleave(nc.vector.tensor_copy, [wg_high], 0, 1, "grouped_high0")
            + interleave(nc.vector.tensor_copy, [wg_high], 1, 2, "grouped_high1")
            + interleave(nc.scalar.copy, [wg_high], 2, TILES, "grouped_high23"),
            P // 2,
        )

        wv = keep.tile([P, 2 * N], U8, align_bytes=64)
        ws = keep.tile([P, N], U8, align_bytes=64)
        nc.vector.tensor_copy(
            wv[:].bitcast(I32).rearrange("p (b a w) -> p b a w", b=TILES, w=2),
            wv_words_raw.rearrange("p (a b w) -> p b a w", b=TILES, w=2),
        )
        nc.vector.tensor_copy(
            ws[:].bitcast(I32).rearrange("p (b a) -> p b a", b=TILES),
            wv_scales_raw.rearrange("p (a b) -> p b a", b=TILES),
        )

        def product(acc, lhsT, lhsT_scale, cols):
            nc.tensor.matmul_mx(
                out=acc,
                lhsT=lhsT,
                lhsT_scale=lhsT_scale,
                rhs=xt[:, cols].bitcast(FP8X4),
                rhs_scale=xs[:, cols],
                start=True,
                stop=True,
            )

        def gate_product(acc, b, cols):
            product(acc, wg_codes[b][:].bitcast(FP8X4), wg_scales[b][:], cols)

        def value_product(acc, b, cols):
            product(acc, wv[:, 2 * P * b : 2 * P * (b + 1)].bitcast(FP4X4), ws[:, P * b : P * (b + 1)], cols)

        half = T // 2
        g0_low = psum.tile([P, T], F32, name="g0_low", tag="shared_bank")
        g0_high = psum.tile([P, T], F32, name="g0_high")
        gate_product(g0_low[:, 0:half], 0, slice(0, half))
        gate_product(g0_high[:, 0:half], 0, slice(half, T))
        g0 = keep.tile([P, WINDOW], F32, name="g0", tag="g_even", align_bytes=64)
        nc.scalar.copy(g0[:, 0:half], g0_low[:, 0:half])
        nc.scalar.copy(g0[:, half:T], g0_high[:, 0:half])

        def gate_bank(b, tag):
            acc = psum.tile([P, T], F32, name=f"g_acc{b}", tag=tag)
            gate_product(acc[:], b, slice(0, T))
            return acc

        def value_bank(b, tag):
            acc = psum.tile([P, T], F32, name=f"v_acc{b}", tag=tag)
            value_product(acc[:], b, slice(0, T))
            return acc

        def window(copy, acc, name, tag):
            tile = keep.tile([P, WINDOW], F32, name=name, tag=tag, align_bytes=64)
            copy(tile[:, 0:T], acc[:])
            return tile

        out_rows = out.rearrange("(a b c) j -> b a c j", b=TILES, c=RUN)

        def gather_gate(g, b, j0, width):
            gate = keep.tile([P, width], F32, name=f"gate{b}_{j0}")
            nc.scalar.activation(gate[:], g[:].indirect(gate_list[:, j0 // 16 : (j0 + width) // 16]), SIGMOID)
            return gate

        def gather_value(v, gate, b, j0, width):
            y = keep.tile([P, width], F32, name=f"y{b}_{j0}")
            nc.vector.tensor_tensor(y[:], v[:].indirect(value_list[:, j0 // 16 : (j0 + width) // 16]), gate[:], MULT)
            nc.sync.dma_start(out_rows[b, :, :, j0 : j0 + width], y[:])

        g1 = window(nc.vector.tensor_copy, gate_bank(1, "g_acc1"), "g1", "g_odd")
        v = [window(nc.vector.tensor_copy, value_bank(b, f"v_acc{b}"), f"v{b}", f"v{b}") for b in range(3)]
        gate0 = gather_gate(g0, 0, 0, J)
        gate1 = gather_gate(g1, 1, 0, J)
        gather_value(v[0], gate0, 0, 0, J)
        g2 = window(nc.scalar.copy, gate_bank(2, "v_acc0"), "g2", "g_even")
        g3 = window(nc.scalar.copy, gate_bank(3, "v_acc1"), "g3", "g_odd")
        gather_value(v[1], gate1, 1, 0, J)
        gate2 = gather_gate(g2, 2, 0, J)
        v3 = window(nc.scalar.copy, value_bank(3, "v_acc2"), "v3", "v0")
        gather_value(v[2], gate2, 2, 0, J)
        for j0 in (0, half):
            gather_value(v3, gather_gate(g3, 3, j0, half), 3, j0, half)
